import numpy as np
import ml_dtypes


def mxq(x, axis, fmt="e4m3"):
    dtype, down = {"e4m3": (ml_dtypes.float8_e4m3fn, 7), "e5m2": (ml_dtypes.float8_e5m2, 14)}[fmt]
    v = np.moveaxis(np.asarray(x, np.float32).astype(ml_dtypes.bfloat16).astype(np.float64), axis, -1)
    blocks = v.reshape(v.shape[:-1] + (-1, 32))
    amax = np.abs(blocks).max(-1, keepdims=True)
    byte = np.maximum(np.where(amax > 0, np.frexp(amax)[1] - 1 + 127, 0) - down, 1)
    scale = np.exp2(byte - 127.0)
    codes = (blocks / scale).astype(np.float32).astype(dtype).astype(np.float64)
    return np.moveaxis((codes * scale).reshape(v.shape), -1, axis)


WIDE = False


def mx_kscale(k):
    if not WIDE:
        return np.ones(k)
    levels = np.array([10, -10, 5, -5, 0])
    if k % 512:
        return np.exp2(np.random.permutation(np.resize(levels, k // 32))).repeat(32)
    a = np.empty((k // 512, 16))
    for p in range(k // 512):
        a[p, :8] = np.random.permutation(np.resize(levels, 8))
        for g in range(8):
            far = levels[np.abs(levels - a[p, g]) >= 10]
            a[p, g + 8] = far[np.random.randint(len(far))]
    return np.exp2(a.ravel()).repeat(32)


def f64(x):
    return np.asarray(x).astype(np.float64)


def striped(idx):
    return np.tile(idx.reshape(-1, 16).T, (8, 1)).astype(np.uint16)


def unstriped(offs):
    return offs[:16].T.reshape(-1).astype(np.int64)


E2M1 = np.array([0.0, 0.5, 1.0, 1.5, 2.0, 3.0, 4.0, 6.0, -0.0, -0.5, -1.0, -1.5, -2.0, -3.0, -4.0, -6.0])


def pack_weight(w, fmt):
    k, n = w.shape
    w = f64(np.asarray(w, np.float32).astype(ml_dtypes.bfloat16)).reshape(k // 32, 32, n)
    amax = np.abs(w).max(1)
    if fmt == "e4m3":
        byte = np.frexp(amax)[1] - 1 + 127 - 7
    else:
        mant, ex = np.frexp(amax / 6.0)
        byte = np.where(mant > 0.5, ex, ex - 1) + 127
    byte = np.clip(np.where(amax > 0, byte, 1), 1, 254)
    scaled = (w * np.exp2(127.0 - byte)[:, None, :]).reshape(k, n).astype(np.float32)
    by_word = np.ascontiguousarray(scaled.reshape(k // 512, 128, 4, n).transpose(0, 1, 3, 2))
    if fmt == "e4m3":
        words = by_word.astype(ml_dtypes.float8_e4m3fn).view(np.uint8)
    else:
        c = by_word.astype(ml_dtypes.float4_e2m1fn).view(np.uint8) & 0xF
        words = (c[..., 0::2] | (c[..., 1::2] << 4)).reshape(k // 512, 128, 2 * n)
    return np.ascontiguousarray(words), np.ascontiguousarray(byte.astype(np.uint8).reshape(k // 512, 16, n))


def unpack_weight(words, scales, fmt):
    g, _, n = scales.shape
    words = np.ascontiguousarray(words).reshape(g, 128, n, -1)
    if fmt == "e4m3":
        vals = words.view(ml_dtypes.float8_e4m3fn).astype(np.float64)
    else:
        nib = np.empty((g, 128, n, 4), np.uint8)
        nib[..., 0::2] = words & 0xF
        nib[..., 1::2] = words >> 4
        vals = E2M1[nib]
    vals = vals * np.repeat(np.exp2(scales.astype(np.float64) - 127.0), 8, axis=1)[..., None]
    return vals.transpose(0, 1, 3, 2).reshape(g * 512, n)


def gelu(v):
    return 0.5 * v * (1.0 + np.tanh(np.sqrt(2.0 / np.pi) * (v + 0.044715 * v**3)))


def striped8(idx):
    return np.concatenate([v.reshape(-1, 16).T for v in idx]).astype(np.uint16)


def unstriped8(offs):
    return np.stack([offs[16 * g:16 * g + 16].T.reshape(-1) for g in range(8)]).astype(np.int64)


def heads(h, wgt, idx8):
    r = np.arange(h.shape[0])
    return wgt[r // 4 % 128] * h[r[:, None], idx8[r % 512 // 64]]


def put_heads(h, wgs, idx8, t2):
    r = np.arange(h.shape[0])
    page = np.zeros((h.shape[0], t2))
    page[r[:, None], idx8[r % 512 // 64]] = wgs[r // 4 % 128] * h
    return page


K, T, H, S, P, T2, N = 1024, 2048, 512, 1024, 1024, 2048, 384

def setup_inputs():
    n = np.random.standard_normal
    s = mx_kscale(K)[:, None]
    u = mx_kscale(H)[:, None]
    d = {}
    d["tab_words"], d["tab_scales"] = pack_weight(n((K, T)) * s, "e4m3")
    d["offs"] = striped(np.random.permutation(T)[:S])
    d["offs2"] = striped8(np.stack([np.random.permutation(T2)[:S] for _ in range(8)]))
    d["offs3"] = striped8(np.stack([np.random.permutation(T2)[:P] for _ in range(8)]))
    d["w1"] = (1.8 * n((K, H)) / np.sqrt(K) / s).astype(np.float32)
    d["w2_words"], d["w2_scales"] = pack_weight(1.8 * n((K, H)) / np.sqrt(K) / s, "e2m1")
    d["gain"] = (np.exp(0.3 * n(H)) * u[:, 0]).astype(np.float32)
    d["wgs"] = np.repeat(np.random.uniform(0.5, 2.0, (8, S)), 16, axis=0).astype(np.float32)
    d["wgt"] = np.repeat(np.random.uniform(0.5, 2.0, (8, P)), 16, axis=0).astype(np.float32)
    d["pressure"] = (n((H, P)) * u).astype(np.float32)
    d["w3"] = (1.2 * n((H, N)) / np.sqrt(H) / u).astype(np.float32)
    d["w4_words"], d["w4_scales"] = pack_weight(0.9 * n((K, N)) / np.sqrt(K) / s, "e2m1")
    d["least"] = (0.5 * n((N, P))).astype(np.float32)
    return d

def reference(tab_words, tab_scales, offs, offs2, offs3, w1, w2_words, w2_scales, gain, wgs, wgt, pressure, w3, w4_words, w4_scales, least):
    v = unpack_weight(tab_words, tab_scales, "e4m3")[:, unstriped(offs)]
    a = mxq(f64(w1), 0, "e4m3").T @ v
    b = unpack_weight(w2_words, w2_scales, "e2m1").T @ v
    h = f64(gain)[:, None] * (np.tanh(a) + np.tanh(b))
    page = put_heads(h, f64(wgs), unstriped8(offs2), T2)
    x = heads(page, f64(wgt), unstriped8(offs3))
    z = mxq(np.maximum(x, f64(pressure)), 0, "e4m3")
    y = mxq(f64(w3), 0, "e4m3").T @ z + unpack_weight(w4_words, w4_scales, "e2m1").T @ v
    return np.maximum(y / (1.0 + np.exp(-y)), f64(least))

@@ -1,0 +1,212 @@
+from contextlib import ExitStack
+
+import concourse.mybir as mybir
+from concourse.masks import make_identity
+
+K, T, H, S, T2, N = 1024, 2048, 512, 1024, 2048, 384
+FLOPS = 2 * S * (2 * K * H + H * N + K * N)
+
+F32 = mybir.dt.float32
+BF16 = mybir.dt.bfloat16
+I32 = mybir.dt.int32
+U32 = mybir.dt.uint32
+U16 = mybir.dt.uint16
+U8 = mybir.dt.uint8
+E4M3 = mybir.dt.float8_e4m3fn_x4
+E2M1 = mybir.dt.float4_e2m1fn_x4
+ACT = mybir.ActivationFunctionType
+ALU = mybir.AluOpType
+
+P = 128
+PACK = 4
+PASSES = K // (P * PACK)
+CHUNK = 256
+CHUNKS = S // CHUNK
+PUT_CHUNKS = ((0, 128), (128, 128), (256, 256), (512, 512))
+LIST_ROWS = 16
+N_TILES = N // P
+
+
+def list_slice(offsets, first, count):
+    return offsets[:, first // LIST_ROWS : (first + count) // LIST_ROWS]
+
+
+def load_scale_rows(nc, plane, scales):
+    for q in range(4):
+        nc.sync.dma_start(
+            out=plane[32 * q : 32 * q + 4, :, :].bitcast(I32),
+            in_=scales[:, 4 * q : 4 * q + 4, :].rearrange("a r c -> r a c").bitcast(I32),
+        )
+
+
+def round_and_interleave(nc, out, in_):
+    nc.scalar.copy(
+        out=out.rearrange("p (c i) t -> p c t i", i=4),
+        in_=in_.rearrange("p t (c i) -> p c t i", i=4),
+    )
+
+
+def tile_list_checkout_scenario_features_kernel(
+    tc, tab_words, tab_scales, offs, offs2, offs3, w1, w2_words, w2_scales, gain, wgs, wgt,
+    pressure, w3, w4_words, w4_scales, least, out,
+):
+    nc = tc.nc
+    with ExitStack() as ctx:
+        keep = ctx.enter_context(tc.tile_pool(name="keep", bufs=1))
+        stage = ctx.enter_context(tc.tile_pool(name="stage", bufs=2))
+        ring = ctx.enter_context(tc.tile_pool(name="ring", bufs=3))
+        psum = ctx.enter_context(tc.psum_pool(name="psum", bufs=1))
+
+        banks = [psum.tile([P, 512], F32, name="bank%d" % b) for b in range(8)]
+
+        idx = keep.tile([P, S // LIST_ROWS], U16)
+        idx2 = keep.tile([P, S // LIST_ROWS], U16)
+        idx3 = keep.tile([P, S // LIST_ROWS], U16)
+        tab_plane = keep.tile([P, PASSES, T], U8, align_bytes=64)
+        w2_plane = keep.tile([P, PASSES, H], U8, align_bytes=64)
+        w4_plane = keep.tile([P, PASSES, N], U8, align_bytes=64)
+        for plane in (tab_plane, w2_plane, w4_plane):
+            nc.vector.memset(plane[:].bitcast(I32), 0)
+        pages = [keep.tile([P, T2], F32, name="page%d" % i) for i in range(PACK)]
+        for page in pages:
+            for first in range(0, T2, 1024):
+                nc.gpsimd.memset(page[:, first : first + 1024], 0.0)
+        ident = keep.tile([P, P], F32)
+        make_identity(nc, ident[:])
+
+        tab = [keep.tile([P, T], U32, name="tab%d" % a) for a in range(PASSES)]
+        w1_raw = [stage.tile([P, PACK, H], F32, name="w1_raw%d" % a, tag="staged") for a in range(PASSES)]
+        w2_codes = keep.tile([P, PASSES, 2 * H], U8, align_bytes=64)
+        w4_codes = keep.tile([P, PASSES, 2 * N], U8, align_bytes=64)
+        gain_sb = keep.tile([P, PACK], F32)
+        wgs_sb = keep.tile([P, S], F32)
+        wgt_sb = keep.tile([P, S], F32)
+        w3_raw = keep.tile([P, PACK, N], F32)
+        least_sb = keep.tile([P, N_TILES, S], F32)
+
+        def load_w1(a):
+            nc.sync.dma_start(out=w1_raw[a][:], in_=w1[512 * a : 512 * (a + 1), :].rearrange("(p t) r -> p t r", t=PACK))
+
+        def load_tab(a):
+            nc.sync.dma_start(out=tab[a][:].bitcast(I32), in_=tab_words[a].rearrange("p t i -> p (t i)").bitcast(I32))
+
+        load_w1(0)
+        load_scale_rows(nc, tab_plane, tab_scales)
+        nc.sync.dma_start(idx[:], offs)
+        load_tab(0)
+        nc.sync.dma_start(out=w2_codes[:].bitcast(I32), in_=w2_words.rearrange("a p c -> p a c").bitcast(I32))
+        load_scale_rows(nc, w2_plane, w2_scales)
+        load_w1(1)
+        load_tab(1)
+        nc.sync.dma_start(out=gain_sb[:], in_=gain.rearrange("(p t) -> p t", t=PACK))
+        nc.sync.dma_start(idx2[:], offs2)
+        nc.sync.dma_start(out=wgs_sb[:], in_=wgs)
+        nc.sync.dma_start(out=w4_codes[:].bitcast(I32), in_=w4_words.rearrange("a p c -> p a c").bitcast(I32))
+        load_scale_rows(nc, w4_plane, w4_scales)
+        nc.sync.dma_start(idx3[:], offs3)
+        nc.sync.dma_start(out=wgt_sb[:], in_=wgt)
+        nc.sync.dma_start(out=least_sb[:], in_=least.rearrange("(t p) j -> p t j", p=P))
+        nc.sync.dma_start(out=w3_raw[:], in_=w3.rearrange("(p t) n -> p t n", t=PACK))
+
+        v_codes = [keep.tile([P, S], U32, name="v_codes%d" % a, align_bytes=64) for a in range(PASSES)]
+        v_plane = [keep.tile([P, S], U8, name="v_plane%d" % a, align_bytes=64) for a in range(PASSES)]
+        for a in range(PASSES):
+            nc.vector.tensor_copy(v_plane[a][:], tab_plane[:, a, :].indirect(idx[:]))
+
+        w1_codes = [keep.tile([P, H], U32, name="w1_codes%d" % a, align_bytes=64) for a in range(PASSES)]
+        w1_plane = [keep.tile([P, H], U8, name="w1_plane%d" % a, align_bytes=64) for a in range(PASSES)]
+        for a in range(PASSES):
+            w1_bf = stage.tile([P, H, PACK], BF16, align_bytes=64)
+            round_and_interleave(nc, w1_bf[:], w1_raw[a][:])
+            nc.vector.quantize_mx(out=w1_codes[a][:].bitcast(E4M3), scales=w1_plane[a][:], in_=w1_bf[:].rearrange("p r t -> p (r t)"))
+            for first, count in ((0, 256), (256, 768)):
+                nc.vector.tensor_copy(v_codes[a][:, first : first + count], tab[a][:].indirect(list_slice(idx, first, count)))
+
+        h = [keep.tile([P, S], F32, name="h%d" % i) for i in range(PACK)]
+        for first, width in PUT_CHUNKS:
+            cols = slice(first, first + width)
+
+            def h_place(i):
+                at = (PACK * first + i * width) % (4 * 512)
+                return banks[4 + at // 512][:, at % 512 : at % 512 + width]
+
+            for jj in range(width // P):
+                j_cols = slice(first + jj * P, first + (jj + 1) * P)
+                turn = (first // P + jj) % 2
+                bank_a, bank_b = banks[turn], banks[2 + turn]
+                for a in range(PASSES):
+                    nc.tensor.matmul_mx(
+                        out=bank_b[:], lhsT=v_codes[a][:, j_cols].bitcast(E4M3), lhsT_scale=v_plane[a][:, j_cols],
+                        rhs=w2_codes[:, a, :].bitcast(E2M1), rhs_scale=w2_plane[:, a, :],
+                        start=(a == 0), stop=(a == PASSES - 1),
+                    )
+                    nc.tensor.matmul_mx(
+                        out=bank_a[:], lhsT=v_codes[a][:, j_cols].bitcast(E4M3), lhsT_scale=v_plane[a][:, j_cols],
+                        rhs=w1_codes[a][:].bitcast(E4M3), rhs_scale=w1_plane[a][:],
+                        start=(a == 0), stop=(a == PASSES - 1),
+                    )
+                tanh_b = ring.tile([P, PACK, P], F32)
+                tanh_a = ring.tile([P, PACK, P], F32)
+                nc.scalar.activation(out=tanh_b[:], in_=bank_b[:].rearrange("j (p t) -> j t p", t=PACK), func=ACT.Tanh)
+                nc.scalar.activation(out=tanh_a[:], in_=bank_a[:].rearrange("j (p t) -> j t p", t=PACK), func=ACT.Tanh)
+                for i in range(PACK):
+                    place = h_place(i)[:, jj * P : (jj + 1) * P]
+                    nc.tensor.matmul(place, tanh_b[:, i, :], ident[:], start=True, stop=False, is_transpose=True)
+                    nc.tensor.matmul(place, tanh_a[:, i, :], ident[:], start=False, stop=True, is_transpose=True)
+            for i in range(PACK):
+                nc.scalar.activation(out=h[i][:, cols], in_=h_place(i), func=ACT.Copy, scale=gain_sb[:, i : i + 1])
+                nc.vector.tensor_tensor(pages[i][:].indirect(list_slice(idx2, first, width)), h[i][:, cols], wgs_sb[:, cols], ALU.mult)
+
+        w3_bf = keep.tile([P, N, PACK], BF16, align_bytes=64)
+        w3_codes = keep.tile([P, N], U32, align_bytes=64)
+        w3_plane = keep.tile([P, N], U8, align_bytes=64)
+        round_and_interleave(nc, w3_bf[:], w3_raw[:])
+        for n_cols in (slice(0, 256), slice(256, N)):
+            nc.vector.quantize_mx(out=w3_codes[:, n_cols].bitcast(E4M3), scales=w3_plane[:, n_cols], in_=w3_bf[:, n_cols, :].rearrange("p n t -> p (n t)"))
+
+        pressure_bf = [keep.tile([P, CHUNK, PACK], BF16, name="pressure_bf%d" % c) for c in range(CHUNKS)]
+        for half in range(2):
+            pressure_raw = stage.tile([P, PACK, 512], F32, tag="staged")
+            nc.sync.dma_start(out=pressure_raw[:], in_=pressure[:, 512 * half : 512 * (half + 1)].rearrange("(p t) j -> p t j", t=PACK))
+            for cc in range(2):
+                round_and_interleave(nc, pressure_bf[2 * half + cc][:], pressure_raw[:, :, cc * CHUNK : (cc + 1) * CHUNK])
+
+        def y_place(c, t):
+            return banks[2 * c + t // 2][:, (t % 2) * CHUNK : (t % 2 + 1) * CHUNK]
+
+        for c in range(CHUNKS):
+            for t in range(N_TILES):
+                for a in range(PASSES):
+                    for jj in range(CHUNK // P):
+                        j_cols = slice(c * CHUNK + jj * P, c * CHUNK + (jj + 1) * P)
+                        nc.tensor.matmul_mx(
+                            out=y_place(c, t)[:, jj * P : (jj + 1) * P],
+                            lhsT=w4_codes[:, a, 2 * P * t : 2 * P * (t + 1)].bitcast(E2M1), lhsT_scale=w4_plane[:, a, P * t : P * (t + 1)],
+                            rhs=v_codes[a][:, j_cols].bitcast(E4M3), rhs_scale=v_plane[a][:, j_cols],
+                            start=(t % 2 == 0 and a == 0 and jj == 0), stop=False,
+                        )
+
+        for c in range(CHUNKS):
+            cols = slice(c * CHUNK, (c + 1) * CHUNK)
+            x = stage.tile([P, PACK, CHUNK], F32)
+            for i in range(PACK):
+                nc.vector.tensor_tensor(x[:, i, :], pages[i][:].indirect(list_slice(idx3, c * CHUNK, CHUNK)), wgt_sb[:, cols], ALU.mult)
+            x_bf = stage.tile([P, CHUNK, PACK], BF16)
+            round_and_interleave(nc, x_bf[:], x[:])
+            z_bf = stage.tile([P, CHUNK * PACK], BF16, align_bytes=64)
+            nc.vector.tensor_tensor(z_bf[:], x_bf[:].rearrange("p j t -> p (j t)"), pressure_bf[c][:].rearrange("p j t -> p (j t)"), ALU.max)
+            z_codes = stage.tile([P, CHUNK], U32, align_bytes=64)
+            z_plane = stage.tile([P, CHUNK], U8, align_bytes=64)
+            nc.vector.quantize_mx(out=z_codes[:].bitcast(E4M3), scales=z_plane[:], in_=z_bf[:])
+            for t in range(N_TILES):
+                n_cols = slice(P * t, P * (t + 1))
+                nc.tensor.matmul_mx(
+                    out=y_place(c, t), lhsT=w3_codes[:, n_cols].bitcast(E4M3), lhsT_scale=w3_plane[:, n_cols],
+                    rhs=z_codes[:].bitcast(E4M3), rhs_scale=z_plane[:],
+                    start=False, stop=(t != 0),
+                )
+            result = ring.tile([P, N_TILES, CHUNK], F32)
+            nc.scalar.activation(out=result[:, 0:2, :].rearrange("p t j -> p (t j)"), in_=banks[2 * c][:], func=ACT.Silu)
+            nc.scalar.activation(out=result[:, 2, :], in_=y_place(c, 2), func=ACT.Silu)
+            nc.vector.tensor_tensor(result[:], result[:], least_sb[:, :, cols], ALU.max)
+            nc.sync.dma_start(out=out[:, cols].rearrange("(t p) j -> p t j", p=P), in_=result[:])

@@ -23,6 +23,7 @@ PASSES = K // (P * PACK)
 CHUNK = 256
 CHUNKS = S // CHUNK
 PUT_CHUNKS = ((0, 128), (128, 128), (256, 256), (512, 512))
+PICK_CHUNKS = ((0, 256, 0), (256, 256, 2), (512, 256, 4), (768, 128, 6), (896, 128, 7))
 LIST_ROWS = 16
 N_TILES = N // P
 
@@ -69,10 +70,12 @@ def tile_list_checkout_scenario_features_kernel(
             nc.vector.memset(plane[:].bitcast(I32), 0)
         pages = [keep.tile([P, T2], F32, name="page%d" % i) for i in range(PACK)]
         for page in pages:
-            for first in range(0, T2, 1024):
-                nc.gpsimd.memset(page[:, first : first + 1024], 0.0)
+            nc.vector.memset(page[:].bitcast(I32), 0)
         ident = keep.tile([P, P], F32)
         make_identity(nc, ident[:])
+
+        warm = keep.tile([P, 1], F32)
+        nc.scalar.activation(out=warm[:], in_=ident[:, 0:1], func=ACT.Silu)
 
         tab = [keep.tile([P, T], U32, name="tab%d" % a) for a in range(PASSES)]
         w1_raw = [stage.tile([P, PACK, H], F32, name="w1_raw%d" % a, tag="staged") for a in range(PASSES)]
@@ -127,8 +130,7 @@ def tile_list_checkout_scenario_features_kernel(
             cols = slice(first, first + width)
 
             def h_place(i):
-                at = (PACK * first + i * width) % (4 * 512)
-                return banks[4 + at // 512][:, at % 512 : at % 512 + width]
+                return banks[4 + i][:, first % 512 : first % 512 + width]
 
             for jj in range(width // P):
                 j_cols = slice(first + jj * P, first + (jj + 1) * P)
@@ -172,41 +174,47 @@ def tile_list_checkout_scenario_features_kernel(
                 round_and_interleave(nc, pressure_bf[2 * half + cc][:], pressure_raw[:, :, cc * CHUNK : (cc + 1) * CHUNK])
 
         def y_place(c, t):
-            return banks[2 * c + t // 2][:, (t % 2) * CHUNK : (t % 2 + 1) * CHUNK]
+            first, width, bank = PICK_CHUNKS[c]
+            at = t * width
+            return banks[bank + at // 512][:, at % 512 : at % 512 + width]
 
-        for c in range(CHUNKS):
+        for c, (first, width, bank) in enumerate(PICK_CHUNKS):
             for t in range(N_TILES):
                 for a in range(PASSES):
-                    for jj in range(CHUNK // P):
-                        j_cols = slice(c * CHUNK + jj * P, c * CHUNK + (jj + 1) * P)
+                    for jj in range(width // P):
+                        j_cols = slice(first + jj * P, first + (jj + 1) * P)
                         nc.tensor.matmul_mx(
                             out=y_place(c, t)[:, jj * P : (jj + 1) * P],
                             lhsT=w4_codes[:, a, 2 * P * t : 2 * P * (t + 1)].bitcast(E2M1), lhsT_scale=w4_plane[:, a, P * t : P * (t + 1)],
                             rhs=v_codes[a][:, j_cols].bitcast(E4M3), rhs_scale=v_plane[a][:, j_cols],
-                            start=(t % 2 == 0 and a == 0 and jj == 0), stop=False,
+                            start=(t * width % 512 == 0 and a == 0 and jj == 0), stop=False,
                         )
 
-        for c in range(CHUNKS):
-            cols = slice(c * CHUNK, (c + 1) * CHUNK)
-            x = stage.tile([P, PACK, CHUNK], F32)
+        for c, (first, width, bank) in enumerate(PICK_CHUNKS):
+            cols = slice(first, first + width)
+            x = stage.tile([P, PACK, width], F32)
             for i in range(PACK):
-                nc.vector.tensor_tensor(x[:, i, :], pages[i][:].indirect(list_slice(idx3, c * CHUNK, CHUNK)), wgt_sb[:, cols], ALU.mult)
-            x_bf = stage.tile([P, CHUNK, PACK], BF16)
+                nc.vector.tensor_tensor(x[:, i, :], pages[i][:].indirect(list_slice(idx3, first, width)), wgt_sb[:, cols], ALU.mult)
+            x_bf = stage.tile([P, width, PACK], BF16)
             round_and_interleave(nc, x_bf[:], x[:])
-            z_bf = stage.tile([P, CHUNK * PACK], BF16, align_bytes=64)
-            nc.vector.tensor_tensor(z_bf[:], x_bf[:].rearrange("p j t -> p (j t)"), pressure_bf[c][:].rearrange("p j t -> p (j t)"), ALU.max)
-            z_codes = stage.tile([P, CHUNK], U32, align_bytes=64)
-            z_plane = stage.tile([P, CHUNK], U8, align_bytes=64)
+            z_bf = stage.tile([P, width * PACK], BF16, align_bytes=64)
+            bound = pressure_bf[first // CHUNK][:, first % CHUNK : first % CHUNK + width, :]
+            nc.vector.tensor_tensor(z_bf[:], x_bf[:].rearrange("p j t -> p (j t)"), bound.rearrange("p j t -> p (j t)"), ALU.max)
+            z_codes = stage.tile([P, width], U32, align_bytes=64)
+            z_plane = stage.tile([P, width], U8, align_bytes=64)
             nc.vector.quantize_mx(out=z_codes[:].bitcast(E4M3), scales=z_plane[:], in_=z_bf[:])
+            result = ring.tile([P, N_TILES, width], F32)
             for t in range(N_TILES):
                 n_cols = slice(P * t, P * (t + 1))
+                closes = t == N_TILES - 1 or (t + 1) * width % 512 == 0
                 nc.tensor.matmul_mx(
                     out=y_place(c, t), lhsT=w3_codes[:, n_cols].bitcast(E4M3), lhsT_scale=w3_plane[:, n_cols],
                     rhs=z_codes[:].bitcast(E4M3), rhs_scale=z_plane[:],
-                    start=False, stop=(t != 0),
+                    start=False, stop=closes,
                 )
-            result = ring.tile([P, N_TILES, CHUNK], F32)
-            nc.scalar.activation(out=result[:, 0:2, :].rearrange("p t j -> p (t j)"), in_=banks[2 * c][:], func=ACT.Silu)
-            nc.scalar.activation(out=result[:, 2, :], in_=y_place(c, 2), func=ACT.Silu)
+            flat = result[:].rearrange("p t j -> p (t j)")
+            for at in range(0, N_TILES * width, 512):
+                count = min(512, N_TILES * width - at)
+                nc.scalar.activation(out=flat[:, at : at + count], in_=banks[bank + at // 512][:, 0:count], func=ACT.Silu)
             nc.vector.tensor_tensor(result[:], result[:], least_sb[:, :, cols], ALU.max)
             nc.sync.dma_start(out=out[:, cols].rearrange("(t p) j -> p t j", p=P), in_=result[:])

@@ -22,7 +22,7 @@ PACK = 4
 PASSES = K // (P * PACK)
 CHUNK = 256
 CHUNKS = S // CHUNK
-PUT_CHUNKS = ((0, 128), (128, 128), (256, 256), (512, 512))
+PUT_CHUNKS = ((0, 128), (128, 128), (256, 128), (384, 128), (512, 256), (768, 256))
 PICK_CHUNKS = ((0, 256, 0), (256, 256, 2), (512, 256, 4), (768, 128, 6), (896, 128, 7))
 LIST_ROWS = 16
 N_TILES = N // P
@@ -32,9 +32,9 @@ def list_slice(offsets, first, count):
     return offsets[:, first // LIST_ROWS : (first + count) // LIST_ROWS]
 
 
-def load_scale_rows(nc, plane, scales):
+def load_scale_rows(queue, plane, scales):
     for q in range(4):
-        nc.sync.dma_start(
+        queue.dma_start(
             out=plane[32 * q : 32 * q + 4, :, :].bitcast(I32),
             in_=scales[:, 4 * q : 4 * q + 4, :].rearrange("a r c -> r a c").bitcast(I32),
         )
@@ -77,42 +77,41 @@ def tile_list_checkout_scenario_features_kernel(
         warm = keep.tile([P, 1], F32)
         nc.scalar.activation(out=warm[:], in_=ident[:, 0:1], func=ACT.Silu)
 
-        tab = [keep.tile([P, T], U32, name="tab%d" % a) for a in range(PASSES)]
+        tab = keep.tile([P, PASSES, T], U32)
         w1_raw = [stage.tile([P, PACK, H], F32, name="w1_raw%d" % a, tag="staged") for a in range(PASSES)]
         w2_codes = keep.tile([P, PASSES, 2 * H], U8, align_bytes=64)
         w4_codes = keep.tile([P, PASSES, 2 * N], U8, align_bytes=64)
         gain_sb = keep.tile([P, PACK], F32)
         wgs_sb = keep.tile([P, S], F32)
         wgt_sb = keep.tile([P, S], F32)
-        w3_raw = keep.tile([P, PACK, N], F32)
         least_sb = keep.tile([P, N_TILES, S], F32)
 
         def load_w1(a):
             nc.sync.dma_start(out=w1_raw[a][:], in_=w1[512 * a : 512 * (a + 1), :].rearrange("(p t) r -> p t r", t=PACK))
 
         def load_tab(a):
-            nc.sync.dma_start(out=tab[a][:].bitcast(I32), in_=tab_words[a].rearrange("p t i -> p (t i)").bitcast(I32))
+            nc.sync.dma_start(out=tab[:, a, :].bitcast(I32), in_=tab_words[a].rearrange("p t i -> p (t i)").bitcast(I32))
 
-        load_w1(0)
-        load_scale_rows(nc, tab_plane, tab_scales)
         nc.sync.dma_start(idx[:], offs)
         load_tab(0)
-        nc.sync.dma_start(out=w2_codes[:].bitcast(I32), in_=w2_words.rearrange("a p c -> p a c").bitcast(I32))
-        load_scale_rows(nc, w2_plane, w2_scales)
+        load_scale_rows(nc.sync, tab_plane, tab_scales)
+        load_w1(0)
         load_w1(1)
+        nc.sync.dma_start(out=w2_codes[:].bitcast(I32), in_=w2_words.rearrange("a p c -> p a c").bitcast(I32))
+        load_scale_rows(nc.sync, w2_plane, w2_scales)
         load_tab(1)
         nc.sync.dma_start(out=gain_sb[:], in_=gain.rearrange("(p t) -> p t", t=PACK))
         nc.sync.dma_start(idx2[:], offs2)
         nc.sync.dma_start(out=wgs_sb[:], in_=wgs)
         nc.sync.dma_start(out=w4_codes[:].bitcast(I32), in_=w4_words.rearrange("a p c -> p a c").bitcast(I32))
-        load_scale_rows(nc, w4_plane, w4_scales)
+        load_scale_rows(nc.sync, w4_plane, w4_scales)
         nc.sync.dma_start(idx3[:], offs3)
         nc.sync.dma_start(out=wgt_sb[:], in_=wgt)
         nc.sync.dma_start(out=least_sb[:], in_=least.rearrange("(t p) j -> p t j", p=P))
-        nc.sync.dma_start(out=w3_raw[:], in_=w3.rearrange("(p t) n -> p t n", t=PACK))
 
         v_codes = [keep.tile([P, S], U32, name="v_codes%d" % a, align_bytes=64) for a in range(PASSES)]
         v_plane = [keep.tile([P, S], U8, name="v_plane%d" % a, align_bytes=64) for a in range(PASSES)]
+        nc.vector.tensor_copy(v_codes[0][:, 0:256], tab[:, 0, :].indirect(list_slice(idx, 0, 256)))
         for a in range(PASSES):
             nc.vector.tensor_copy(v_plane[a][:], tab_plane[:, a, :].indirect(idx[:]))
 
@@ -122,8 +121,9 @@ def tile_list_checkout_scenario_features_kernel(
             w1_bf = stage.tile([P, H, PACK], BF16, align_bytes=64)
             round_and_interleave(nc, w1_bf[:], w1_raw[a][:])
             nc.vector.quantize_mx(out=w1_codes[a][:].bitcast(E4M3), scales=w1_plane[a][:], in_=w1_bf[:].rearrange("p r t -> p (r t)"))
-            for first, count in ((0, 256), (256, 768)):
-                nc.vector.tensor_copy(v_codes[a][:, first : first + count], tab[a][:].indirect(list_slice(idx, first, count)))
+        nc.vector.tensor_copy(v_codes[1][:, 0:256], tab[:, 1, :].indirect(list_slice(idx, 0, 256)))
+        nc.vector.tensor_copy(v_codes[0][:, 256:S], tab[:].rearrange("p a t -> p (a t)").indirect(list_slice(idx, 256, S - 256)))
+        nc.vector.tensor_copy(v_codes[1][:, 256:S], tab[:, 1, :].indirect(list_slice(idx, 256, S - 256)))
 
         h = [keep.tile([P, S], F32, name="h%d" % i) for i in range(PACK)]
         for first, width in PUT_CHUNKS:
@@ -159,19 +159,21 @@ def tile_list_checkout_scenario_features_kernel(
                 nc.scalar.activation(out=h[i][:, cols], in_=h_place(i), func=ACT.Copy, scale=gain_sb[:, i : i + 1])
                 nc.vector.tensor_tensor(pages[i][:].indirect(list_slice(idx2, first, width)), h[i][:, cols], wgs_sb[:, cols], ALU.mult)
 
-        w3_bf = keep.tile([P, N, PACK], BF16, align_bytes=64)
-        w3_codes = keep.tile([P, N], U32, align_bytes=64)
-        w3_plane = keep.tile([P, N], U8, align_bytes=64)
-        round_and_interleave(nc, w3_bf[:], w3_raw[:])
-        for n_cols in (slice(0, 256), slice(256, N)):
-            nc.vector.quantize_mx(out=w3_codes[:, n_cols].bitcast(E4M3), scales=w3_plane[:, n_cols], in_=w3_bf[:, n_cols, :].rearrange("p n t -> p (n t)"))
-
         pressure_bf = [keep.tile([P, CHUNK, PACK], BF16, name="pressure_bf%d" % c) for c in range(CHUNKS)]
         for half in range(2):
             pressure_raw = stage.tile([P, PACK, 512], F32, tag="staged")
             nc.sync.dma_start(out=pressure_raw[:], in_=pressure[:, 512 * half : 512 * (half + 1)].rearrange("(p t) j -> p t j", t=PACK))
             for cc in range(2):
                 round_and_interleave(nc, pressure_bf[2 * half + cc][:], pressure_raw[:, :, cc * CHUNK : (cc + 1) * CHUNK])
+
+        w3_bf = keep.tile([P, N, PACK], BF16, align_bytes=64)
+        w3_codes = keep.tile([P, N], U32, align_bytes=64)
+        w3_plane = keep.tile([P, N], U8, align_bytes=64)
+        w3_raw = stage.tile([P, PACK, N], F32, tag="staged")
+        nc.sync.dma_start(out=w3_raw[:], in_=w3.rearrange("(p t) n -> p t n", t=PACK))
+        round_and_interleave(nc, w3_bf[:], w3_raw[:])
+        for n_cols in (slice(0, 256), slice(256, N)):
+            nc.vector.quantize_mx(out=w3_codes[:, n_cols].bitcast(E4M3), scales=w3_plane[:, n_cols], in_=w3_bf[:, n_cols, :].rearrange("p n t -> p (n t)"))
 
         def y_place(c, t):
             first, width, bank = PICK_CHUNKS[c]

@@ -63,14 +63,13 @@ def tile_list_checkout_scenario_features_kernel(
         idx = keep.tile([P, S // LIST_ROWS], U16)
         idx2 = keep.tile([P, S // LIST_ROWS], U16)
         idx3 = keep.tile([P, S // LIST_ROWS], U16)
-        tab_plane = keep.tile([P, PASSES, T], U8, align_bytes=64)
+        tab_plane = keep.tile([P, T], U8, align_bytes=64)
+        v_plane = [keep.tile([P, S], U8, name="v_plane%d" % a, align_bytes=64) for a in range(PASSES)]
         w2_plane = keep.tile([P, PASSES, H], U8, align_bytes=64)
         w4_plane = keep.tile([P, PASSES, N], U8, align_bytes=64)
-        for plane in (tab_plane, w2_plane, w4_plane):
+        for plane in (tab_plane, w2_plane, v_plane[1], w4_plane):
             nc.vector.memset(plane[:].bitcast(I32), 0)
         pages = [keep.tile([P, T2], F32, name="page%d" % i) for i in range(PACK)]
-        for page in pages:
-            nc.vector.memset(page[:].bitcast(I32), 0)
         ident = keep.tile([P, P], F32)
         make_identity(nc, ident[:])
 
@@ -94,12 +93,22 @@ def tile_list_checkout_scenario_features_kernel(
 
         nc.sync.dma_start(idx[:], offs)
         load_tab(0)
-        load_scale_rows(nc.sync, tab_plane, tab_scales)
+        for q in range(4):
+            nc.sync.dma_start(out=tab_plane[32 * q : 32 * q + 8, :].bitcast(I32), in_=tab_scales[:, 4 * q : 4 * q + 4, :].bitcast(I32))
         load_w1(0)
         load_w1(1)
         nc.sync.dma_start(out=w2_codes[:].bitcast(I32), in_=w2_words.rearrange("a p c -> p a c").bitcast(I32))
         load_scale_rows(nc.sync, w2_plane, w2_scales)
         load_tab(1)
+
+        v_codes = [keep.tile([P, S], U32, name="v_codes%d" % a, align_bytes=64) for a in range(PASSES)]
+        nc.vector.tensor_copy(v_plane[0][:], tab_plane[:].indirect(idx[:]))
+        for q in range(4):
+            nc.sync.dma_start(out=v_plane[1][32 * q : 32 * q + 4, :].bitcast(I32), in_=v_plane[0][32 * q + 4 : 32 * q + 8, :].bitcast(I32))
+        nc.vector.tensor_copy(v_codes[0][:, 0:256], tab[:, 0, :].indirect(list_slice(idx, 0, 256)))
+        for page in pages:
+            nc.vector.memset(page[:].bitcast(I32), 0)
+
         nc.sync.dma_start(out=gain_sb[:], in_=gain.rearrange("(p t) -> p t", t=PACK))
         nc.sync.dma_start(idx2[:], offs2)
         nc.sync.dma_start(out=wgs_sb[:], in_=wgs)
@@ -109,18 +118,14 @@ def tile_list_checkout_scenario_features_kernel(
         nc.sync.dma_start(out=wgt_sb[:], in_=wgt)
         nc.sync.dma_start(out=least_sb[:], in_=least.rearrange("(t p) j -> p t j", p=P))
 
-        v_codes = [keep.tile([P, S], U32, name="v_codes%d" % a, align_bytes=64) for a in range(PASSES)]
-        v_plane = [keep.tile([P, S], U8, name="v_plane%d" % a, align_bytes=64) for a in range(PASSES)]
-        nc.vector.tensor_copy(v_codes[0][:, 0:256], tab[:, 0, :].indirect(list_slice(idx, 0, 256)))
-        for a in range(PASSES):
-            nc.vector.tensor_copy(v_plane[a][:], tab_plane[:, a, :].indirect(idx[:]))
-
         w1_codes = [keep.tile([P, H], U32, name="w1_codes%d" % a, align_bytes=64) for a in range(PASSES)]
         w1_plane = [keep.tile([P, H], U8, name="w1_plane%d" % a, align_bytes=64) for a in range(PASSES)]
         for a in range(PASSES):
-            w1_bf = stage.tile([P, H, PACK], BF16, align_bytes=64)
-            round_and_interleave(nc, w1_bf[:], w1_raw[a][:])
-            nc.vector.quantize_mx(out=w1_codes[a][:].bitcast(E4M3), scales=w1_plane[a][:], in_=w1_bf[:].rearrange("p r t -> p (r t)"))
+            for half in range(2):
+                r_cols = slice(256 * half, 256 * (half + 1))
+                w1_bf = ring.tile([P, 256, PACK], BF16, align_bytes=64)
+                round_and_interleave(nc, w1_bf[:], w1_raw[a][:, :, r_cols])
+                nc.vector.quantize_mx(out=w1_codes[a][:, r_cols].bitcast(E4M3), scales=w1_plane[a][:, r_cols], in_=w1_bf[:].rearrange("p r t -> p (r t)"))
         nc.vector.tensor_copy(v_codes[1][:, 0:256], tab[:, 1, :].indirect(list_slice(idx, 0, 256)))
         nc.vector.tensor_copy(v_codes[0][:, 256:S], tab[:].rearrange("p a t -> p (a t)").indirect(list_slice(idx, 256, S - 256)))
         nc.vector.tensor_copy(v_codes[1][:, 256:S], tab[:, 1, :].indirect(list_slice(idx, 256, S - 256)))

from contextlib import ExitStack

import concourse.mybir as mybir
from concourse.masks import make_identity

K, T, H, S, T2, N = 1024, 2048, 512, 1024, 2048, 384
FLOPS = 2 * S * (2 * K * H + H * N + K * N)

F32 = mybir.dt.float32
BF16 = mybir.dt.bfloat16
I32 = mybir.dt.int32
U32 = mybir.dt.uint32
U16 = mybir.dt.uint16
U8 = mybir.dt.uint8
E4M3 = mybir.dt.float8_e4m3fn_x4
E2M1 = mybir.dt.float4_e2m1fn_x4
ACT = mybir.ActivationFunctionType
ALU = mybir.AluOpType

P = 128
PACK = 4
PASSES = K // (P * PACK)
CHUNK = 256
CHUNKS = S // CHUNK
PUT_CHUNKS = ((0, 128), (128, 128), (256, 128), (384, 128), (512, 256), (768, 256))
PICK_CHUNKS = ((0, 256, 0), (256, 256, 2), (512, 256, 4), (768, 128, 6), (896, 128, 7))
LIST_ROWS = 16
N_TILES = N // P


def list_slice(offsets, first, count):
    return offsets[:, first // LIST_ROWS : (first + count) // LIST_ROWS]


def load_scale_rows(queue, plane, scales):
    for q in range(4):
        queue.dma_start(
            out=plane[32 * q : 32 * q + 4, :, :].bitcast(I32),
            in_=scales[:, 4 * q : 4 * q + 4, :].rearrange("a r c -> r a c").bitcast(I32),
        )


def round_and_interleave(nc, out, in_):
    nc.scalar.copy(
        out=out.rearrange("p (c i) t -> p c t i", i=4),
        in_=in_.rearrange("p t (c i) -> p c t i", i=4),
    )


def tile_list_checkout_scenario_features_kernel(
    tc, tab_words, tab_scales, offs, offs2, offs3, w1, w2_words, w2_scales, gain, wgs, wgt,
    pressure, w3, w4_words, w4_scales, least, out,
):
    nc = tc.nc
    with ExitStack() as ctx:
        keep = ctx.enter_context(tc.tile_pool(name="keep", bufs=1))
        stage = ctx.enter_context(tc.tile_pool(name="stage", bufs=2))
        ring = ctx.enter_context(tc.tile_pool(name="ring", bufs=3))
        psum = ctx.enter_context(tc.psum_pool(name="psum", bufs=1))

        banks = [psum.tile([P, 512], F32, name="bank%d" % b) for b in range(8)]

        idx = keep.tile([P, S // LIST_ROWS], U16)
        idx2 = keep.tile([P, S // LIST_ROWS], U16)
        idx3 = keep.tile([P, S // LIST_ROWS], U16)
        tab_plane = keep.tile([P, T], U8, align_bytes=64)
        v_plane = [keep.tile([P, S], U8, name="v_plane%d" % a, align_bytes=64) for a in range(PASSES)]
        w2_plane = keep.tile([P, PASSES, H], U8, align_bytes=64)
        w4_plane = keep.tile([P, PASSES, N], U8, align_bytes=64)
        for plane in (tab_plane, w2_plane, v_plane[1], w4_plane):
            nc.vector.memset(plane[:].bitcast(I32), 0)
        pages = [keep.tile([P, T2], F32, name="page%d" % i) for i in range(PACK)]
        ident = keep.tile([P, P], F32)
        make_identity(nc, ident[:])

        warm = keep.tile([P, 1], F32)
        nc.scalar.activation(out=warm[:], in_=ident[:, 0:1], func=ACT.Silu)

        tab = keep.tile([P, PASSES, T], U32)
        w1_raw = [stage.tile([P, PACK, H], F32, name="w1_raw%d" % a, tag="staged") for a in range(PASSES)]
        w2_codes = keep.tile([P, PASSES, 2 * H], U8, align_bytes=64)
        w4_codes = keep.tile([P, PASSES, 2 * N], U8, align_bytes=64)
        gain_sb = keep.tile([P, PACK], F32)
        wgs_sb = keep.tile([P, S], F32)
        wgt_sb = keep.tile([P, S], F32)
        least_sb = keep.tile([P, N_TILES, S], F32)

        def load_w1(a):
            nc.sync.dma_start(out=w1_raw[a][:], in_=w1[512 * a : 512 * (a + 1), :].rearrange("(p t) r -> p t r", t=PACK))

        def load_tab(a):
            nc.sync.dma_start(out=tab[:, a, :].bitcast(I32), in_=tab_words[a].rearrange("p t i -> p (t i)").bitcast(I32))

        nc.sync.dma_start(idx[:], offs)
        load_tab(0)
        for q in range(4):
            nc.sync.dma_start(out=tab_plane[32 * q : 32 * q + 8, :].bitcast(I32), in_=tab_scales[:, 4 * q : 4 * q + 4, :].bitcast(I32))
        load_w1(0)
        load_w1(1)
        nc.sync.dma_start(out=w2_codes[:].bitcast(I32), in_=w2_words.rearrange("a p c -> p a c").bitcast(I32))
        load_scale_rows(nc.sync, w2_plane, w2_scales)
        load_tab(1)

        v_codes = [keep.tile([P, S], U32, name="v_codes%d" % a, align_bytes=64) for a in range(PASSES)]
        nc.vector.tensor_copy(v_plane[0][:], tab_plane[:].indirect(idx[:]))
        for q in range(4):
            nc.sync.dma_start(out=v_plane[1][32 * q : 32 * q + 4, :].bitcast(I32), in_=v_plane[0][32 * q + 4 : 32 * q + 8, :].bitcast(I32))
        nc.vector.tensor_copy(v_codes[0][:, 0:256], tab[:, 0, :].indirect(list_slice(idx, 0, 256)))
        for page in pages:
            nc.vector.memset(page[:].bitcast(I32), 0)

        nc.sync.dma_start(out=gain_sb[:], in_=gain.rearrange("(p t) -> p t", t=PACK))
        nc.sync.dma_start(idx2[:], offs2)
        nc.sync.dma_start(out=wgs_sb[:], in_=wgs)
        nc.sync.dma_start(out=w4_codes[:].bitcast(I32), in_=w4_words.rearrange("a p c -> p a c").bitcast(I32))
        load_scale_rows(nc.sync, w4_plane, w4_scales)
        nc.sync.dma_start(idx3[:], offs3)
        nc.sync.dma_start(out=wgt_sb[:], in_=wgt)
        nc.sync.dma_start(out=least_sb[:], in_=least.rearrange("(t p) j -> p t j", p=P))

        w1_codes = [keep.tile([P, H], U32, name="w1_codes%d" % a, align_bytes=64) for a in range(PASSES)]
        w1_plane = [keep.tile([P, H], U8, name="w1_plane%d" % a, align_bytes=64) for a in range(PASSES)]
        for a in range(PASSES):
            for half in range(2):
                r_cols = slice(256 * half, 256 * (half + 1))
                w1_bf = ring.tile([P, 256, PACK], BF16, align_bytes=64)
                round_and_interleave(nc, w1_bf[:], w1_raw[a][:, :, r_cols])
                nc.vector.quantize_mx(out=w1_codes[a][:, r_cols].bitcast(E4M3), scales=w1_plane[a][:, r_cols], in_=w1_bf[:].rearrange("p r t -> p (r t)"))
        nc.vector.tensor_copy(v_codes[1][:, 0:256], tab[:, 1, :].indirect(list_slice(idx, 0, 256)))
        nc.vector.tensor_copy(v_codes[0][:, 256:S], tab[:].rearrange("p a t -> p (a t)").indirect(list_slice(idx, 256, S - 256)))
        nc.vector.tensor_copy(v_codes[1][:, 256:S], tab[:, 1, :].indirect(list_slice(idx, 256, S - 256)))

        h = [keep.tile([P, S], F32, name="h%d" % i) for i in range(PACK)]
        for first, width in PUT_CHUNKS:
            cols = slice(first, first + width)

            def h_place(i):
                return banks[4 + i][:, first % 512 : first % 512 + width]

            for jj in range(width // P):
                j_cols = slice(first + jj * P, first + (jj + 1) * P)
                turn = (first // P + jj) % 2
                bank_a, bank_b = banks[turn], banks[2 + turn]
                for a in range(PASSES):
                    nc.tensor.matmul_mx(
                        out=bank_b[:], lhsT=v_codes[a][:, j_cols].bitcast(E4M3), lhsT_scale=v_plane[a][:, j_cols],
                        rhs=w2_codes[:, a, :].bitcast(E2M1), rhs_scale=w2_plane[:, a, :],
                        start=(a == 0), stop=(a == PASSES - 1),
                    )
                    nc.tensor.matmul_mx(
                        out=bank_a[:], lhsT=v_codes[a][:, j_cols].bitcast(E4M3), lhsT_scale=v_plane[a][:, j_cols],
                        rhs=w1_codes[a][:].bitcast(E4M3), rhs_scale=w1_plane[a][:],
                        start=(a == 0), stop=(a == PASSES - 1),
                    )
                tanh_b = ring.tile([P, PACK, P], F32)
                tanh_a = ring.tile([P, PACK, P], F32)
                nc.scalar.activation(out=tanh_b[:], in_=bank_b[:].rearrange("j (p t) -> j t p", t=PACK), func=ACT.Tanh)
                nc.scalar.activation(out=tanh_a[:], in_=bank_a[:].rearrange("j (p t) -> j t p", t=PACK), func=ACT.Tanh)
                for i in range(PACK):
                    place = h_place(i)[:, jj * P : (jj + 1) * P]
                    nc.tensor.matmul(place, tanh_b[:, i, :], ident[:], start=True, stop=False, is_transpose=True)
                    nc.tensor.matmul(place, tanh_a[:, i, :], ident[:], start=False, stop=True, is_transpose=True)
            for i in range(PACK):
                nc.scalar.activation(out=h[i][:, cols], in_=h_place(i), func=ACT.Copy, scale=gain_sb[:, i : i + 1])
                nc.vector.tensor_tensor(pages[i][:].indirect(list_slice(idx2, first, width)), h[i][:, cols], wgs_sb[:, cols], ALU.mult)

        pressure_bf = [keep.tile([P, CHUNK, PACK], BF16, name="pressure_bf%d" % c) for c in range(CHUNKS)]
        for half in range(2):
            pressure_raw = stage.tile([P, PACK, 512], F32, tag="staged")
            nc.sync.dma_start(out=pressure_raw[:], in_=pressure[:, 512 * half : 512 * (half + 1)].rearrange("(p t) j -> p t j", t=PACK))
            for cc in range(2):
                round_and_interleave(nc, pressure_bf[2 * half + cc][:], pressure_raw[:, :, cc * CHUNK : (cc + 1) * CHUNK])

        w3_bf = keep.tile([P, N, PACK], BF16, align_bytes=64)
        w3_codes = keep.tile([P, N], U32, align_bytes=64)
        w3_plane = keep.tile([P, N], U8, align_bytes=64)
        w3_raw = stage.tile([P, PACK, N], F32, tag="staged")
        nc.sync.dma_start(out=w3_raw[:], in_=w3.rearrange("(p t) n -> p t n", t=PACK))
        round_and_interleave(nc, w3_bf[:], w3_raw[:])
        for n_cols in (slice(0, 256), slice(256, N)):
            nc.vector.quantize_mx(out=w3_codes[:, n_cols].bitcast(E4M3), scales=w3_plane[:, n_cols], in_=w3_bf[:, n_cols, :].rearrange("p n t -> p (n t)"))

        def y_place(c, t):
            first, width, bank = PICK_CHUNKS[c]
            at = t * width
            return banks[bank + at // 512][:, at % 512 : at % 512 + width]

        for c, (first, width, bank) in enumerate(PICK_CHUNKS):
            for t in range(N_TILES):
                for a in range(PASSES):
                    for jj in range(width // P):
                        j_cols = slice(first + jj * P, first + (jj + 1) * P)
                        nc.tensor.matmul_mx(
                            out=y_place(c, t)[:, jj * P : (jj + 1) * P],
                            lhsT=w4_codes[:, a, 2 * P * t : 2 * P * (t + 1)].bitcast(E2M1), lhsT_scale=w4_plane[:, a, P * t : P * (t + 1)],
                            rhs=v_codes[a][:, j_cols].bitcast(E4M3), rhs_scale=v_plane[a][:, j_cols],
                            start=(t * width % 512 == 0 and a == 0 and jj == 0), stop=False,
                        )

        for c, (first, width, bank) in enumerate(PICK_CHUNKS):
            cols = slice(first, first + width)
            x = stage.tile([P, PACK, width], F32)
            for i in range(PACK):
                nc.vector.tensor_tensor(x[:, i, :], pages[i][:].indirect(list_slice(idx3, first, width)), wgt_sb[:, cols], ALU.mult)
            x_bf = stage.tile([P, width, PACK], BF16)
            round_and_interleave(nc, x_bf[:], x[:])
            z_bf = stage.tile([P, width * PACK], BF16, align_bytes=64)
            bound = pressure_bf[first // CHUNK][:, first % CHUNK : first % CHUNK + width, :]
            nc.vector.tensor_tensor(z_bf[:], x_bf[:].rearrange("p j t -> p (j t)"), bound.rearrange("p j t -> p (j t)"), ALU.max)
            z_codes = stage.tile([P, width], U32, align_bytes=64)
            z_plane = stage.tile([P, width], U8, align_bytes=64)
            nc.vector.quantize_mx(out=z_codes[:].bitcast(E4M3), scales=z_plane[:], in_=z_bf[:])
            result = ring.tile([P, N_TILES, width], F32)
            for t in range(N_TILES):
                n_cols = slice(P * t, P * (t + 1))
                closes = t == N_TILES - 1 or (t + 1) * width % 512 == 0
                nc.tensor.matmul_mx(
                    out=y_place(c, t), lhsT=w3_codes[:, n_cols].bitcast(E4M3), lhsT_scale=w3_plane[:, n_cols],
                    rhs=z_codes[:].bitcast(E4M3), rhs_scale=z_plane[:],
                    start=False, stop=closes,
                )
            flat = result[:].rearrange("p t j -> p (t j)")
            for at in range(0, N_TILES * width, 512):
                count = min(512, N_TILES * width - at)
                nc.scalar.activation(out=flat[:, at : at + count], in_=banks[bank + at // 512][:, 0:count], func=ACT.Silu)
            nc.vector.tensor_tensor(result[:], result[:], least_sb[:, :, cols], ALU.max)
            nc.sync.dma_start(out=out[:, cols].rearrange("(t p) j -> p t j", p=P), in_=result[:])
